import numpy as np
import ml_dtypes


def mxq(x, axis, fmt="e4m3"):
    dtype, down = {"e4m3": (ml_dtypes.float8_e4m3fn, 7), "e5m2": (ml_dtypes.float8_e5m2, 14)}[fmt]
    v = np.moveaxis(np.asarray(x, np.float32).astype(ml_dtypes.bfloat16).astype(np.float64), axis, -1)
    blocks = v.reshape(v.shape[:-1] + (-1, 32))
    amax = np.abs(blocks).max(-1, keepdims=True)
    byte = np.maximum(np.where(amax > 0, np.frexp(amax)[1] - 1 + 127, 0) - down, 1)
    scale = np.exp2(byte - 127.0)
    codes = (blocks / scale).astype(np.float32).astype(dtype).astype(np.float64)
    return np.moveaxis((codes * scale).reshape(v.shape), -1, axis)


WIDE = False


def mx_kscale(k):
    if not WIDE:
        return np.ones(k)
    levels = np.array([10, -10, 5, -5, 0])
    if k % 512:
        return np.exp2(np.random.permutation(np.resize(levels, k // 32))).repeat(32)
    a = np.empty((k // 512, 16))
    for p in range(k // 512):
        a[p, :8] = np.random.permutation(np.resize(levels, 8))
        for g in range(8):
            far = levels[np.abs(levels - a[p, g]) >= 10]
            a[p, g + 8] = far[np.random.randint(len(far))]
    return np.exp2(a.ravel()).repeat(32)


def f64(x):
    return np.asarray(x).astype(np.float64)


def striped8(idx):
    return np.asarray(idx).reshape(8, -1, 16).transpose(0, 2, 1).reshape(128, -1).astype(np.uint16)


def unstriped8(offs):
    return offs.reshape(8, 16, -1).transpose(0, 2, 1).reshape(8, -1).astype(np.int64)


def pick8(x, idx, run):
    r = np.arange(len(x))
    return x[r[:, None], idx[r % (8 * run) // run]]


E2M1 = np.array([0.0, 0.5, 1.0, 1.5, 2.0, 3.0, 4.0, 6.0, -0.0, -0.5, -1.0, -1.5, -2.0, -3.0, -4.0, -6.0])


def pack_weight(w, fmt):
    k, n = w.shape
    w = f64(np.asarray(w, np.float32).astype(ml_dtypes.bfloat16)).reshape(k // 32, 32, n)
    amax = np.abs(w).max(1)
    if fmt == "e4m3":
        byte = np.frexp(amax)[1] - 1 + 127 - 7
    else:
        mant, ex = np.frexp(amax / 6.0)
        byte = np.where(mant > 0.5, ex, ex - 1) + 127
    byte = np.clip(np.where(amax > 0, byte, 1), 1, 254)
    scaled = (w * np.exp2(127.0 - byte)[:, None, :]).reshape(k, n).astype(np.float32)
    by_word = np.ascontiguousarray(scaled.reshape(k // 512, 128, 4, n).transpose(0, 1, 3, 2))
    if fmt == "e4m3":
        words = by_word.astype(ml_dtypes.float8_e4m3fn).view(np.uint8)
    else:
        c = by_word.astype(ml_dtypes.float4_e2m1fn).view(np.uint8) & 0xF
        words = (c[..., 0::2] | (c[..., 1::2] << 4)).reshape(k // 512, 128, 2 * n)
    return np.ascontiguousarray(words), np.ascontiguousarray(byte.astype(np.uint8).reshape(k // 512, 16, n))


def unpack_weight(words, scales, fmt):
    g, _, n = scales.shape
    words = np.ascontiguousarray(words).reshape(g, 128, n, -1)
    if fmt == "e4m3":
        vals = words.view(ml_dtypes.float8_e4m3fn).astype(np.float64)
    else:
        nib = np.empty((g, 128, n, 4), np.uint8)
        nib[..., 0::2] = words & 0xF
        nib[..., 1::2] = words >> 4
        vals = E2M1[nib]
    vals = vals * np.repeat(np.exp2(scales.astype(np.float64) - 127.0), 8, axis=1)[..., None]
    return vals.transpose(0, 1, 3, 2).reshape(g * 512, n)


D, T, I, Q = 512, 1024, 512, 128


def setup_inputs():
    n = np.random.standard_normal
    idx = np.stack([np.random.permutation(T)[:I] for _ in range(8)])
    idx2 = np.stack([np.random.permutation(T)[:I] for _ in range(8)])
    idx3 = np.stack([np.random.permutation(T)[:I] for _ in range(8)])
    idx4 = np.stack([np.random.permutation(T)[:I] for _ in range(8)])
    fd = mx_kscale(D)
    keysp = pack_weight(n((D, T)) / fd[:, None], "e4m3")
    return {
        "query": (n((D, Q)) * 1.0 / np.sqrt(D) * fd[:, None]).astype(np.float32),
        "keys_words": keysp[0],
        "keys_scales": keysp[1],
        "lam": (np.random.uniform(0.3, 0.9, (Q, 1))).astype(np.float32),
        "old": (1.0 * n((Q, T))).astype(np.float32),
        "offs": striped8(idx),
        "offs2": striped8(idx2),
        "offs3": striped8(idx3),
        "offs4": striped8(idx4),
    }


def reference(query, keys_words, keys_scales, lam, old, offs, offs2, offs3, offs4):
    idx = unstriped8(offs)
    idx2 = unstriped8(offs2)
    idx3 = unstriped8(offs3)
    idx4 = unstriped8(offs4)
    keysu = unpack_weight(keys_words, keys_scales, "e4m3")
    queryq = mxq(f64(query), 0, "e4m3")
    a = queryq.T @ keysu
    rv = np.log(np.exp(pick8(a, idx2, 16)) + np.exp(pick8(a, idx3, 16)))
    w = pick8(a, idx, 16) - rv * f64(lam)
    f1 = np.zeros((Q, T))
    f1[np.arange(Q)[:, None], idx4[np.arange(Q) % 128 // 16]] = w
    y = f64(old) + f1
    return y

@@ -1,0 +1,129 @@
+from contextlib import ExitStack
+
+import concourse.mybir as mybir
+
+F32 = mybir.dt.float32
+BF16 = mybir.dt.bfloat16
+I32 = mybir.dt.int32
+U32 = mybir.dt.uint32
+U16 = mybir.dt.uint16
+U8 = mybir.dt.uint8
+FP8X4 = mybir.dt.float8_e4m3fn_x4
+ALU = mybir.AluOpType
+ACT = mybir.ActivationFunctionType
+
+P = 128
+PACK = 4
+D, T, SLOTS, Q = 512, 1024, 512, 128
+HALF = SLOTS // 2
+GROUP = 16
+N_PASS = 256
+CLAMP = 30.0
+STORE = 256
+
+FLOPS = 2 * D * T * Q
+
+
+def tile_attend_tworivals_lean_putold_heads_kernel(
+    tc, query, keys_words, keys_scales, lam, old, offs, offs2, offs3, offs4, out
+):
+    nc = tc.nc
+    with ExitStack() as ctx:
+        sb = ctx.enter_context(tc.tile_pool(name="sb", bufs=1))
+        ps = ctx.enter_context(tc.psum_pool(name="ps", bufs=1))
+
+        key_plane = sb.tile([P, T], U8, align_bytes=64)
+        nc.vector.memset(key_plane[:].bitcast(I32), 0)
+        window = sb.tile([P, T], F32)
+        nc.vector.memset(window[:], 0.0)
+
+        q_raw = sb.tile([P, PACK, Q], F32)
+        nc.sync.dma_start(out=q_raw[:], in_=query.rearrange("(p j) q -> p j q", j=PACK))
+        words_hbm = keys_words[0].rearrange("p n t -> p (n t)").bitcast(I32)
+        words = [sb.tile([P, T // 2], U32, align_bytes=64, name="words%d" % c) for c in range(2)]
+        for c in range(2):
+            nc.sync.dma_start(out=words[c][:].bitcast(I32), in_=words_hbm[:, c * (T // 2) : (c + 1) * (T // 2)])
+
+        lam_col = sb.tile([P, 1], F32)
+        nc.scalar.dma_start(out=lam_col[:], in_=lam)
+        for quad in range(4):
+            nc.scalar.dma_start(
+                out=key_plane[32 * quad : 32 * quad + 4, :].bitcast(I32),
+                in_=keys_scales[0][4 * quad : 4 * quad + 4, :].bitcast(I32),
+            )
+
+        list3 = sb.tile([P, SLOTS // GROUP], U16)
+        list2 = sb.tile([P, SLOTS // GROUP], U16)
+        list1 = sb.tile([P, SLOTS // GROUP], U16)
+        list4 = sb.tile([P, SLOTS // GROUP], U16)
+        for lst, src in ((list3, offs3), (list2, offs2), (list1, offs), (list4, offs4)):
+            nc.sync.dma_start(lst[:], src)
+        old_sb = sb.tile([P, T], F32)
+        nc.sync.dma_start(out=old_sb[:], in_=old)
+
+        neg_lam = sb.tile([P, 1], F32)
+        nc.scalar.activation(neg_lam[:], lam_col[:], ACT.Copy, scale=-1.0)
+
+        q_grouped = sb.tile([P, Q, PACK], BF16, align_bytes=64)
+        nc.vector.tensor_copy(out=q_grouped[:], in_=q_raw[:].rearrange("p j q -> p q j"))
+        q_codes = sb.tile([P, Q], U32, align_bytes=64)
+        q_plane = sb.tile([P, Q], U8, align_bytes=64)
+        nc.vector.quantize_mx(
+            out=q_codes[:].bitcast(FP8X4), scales=q_plane[:], in_=q_grouped[:].rearrange("p q j -> p (q j)")
+        )
+
+        scores = sb.tile([P, T], F32)
+        for n in range(T // N_PASS):
+            bank = ps.tile([P, N_PASS], F32, name="bank%d" % n)
+            c, first = divmod(n * N_PASS, T // 2)
+            cols = slice(n * N_PASS, (n + 1) * N_PASS)
+            nc.tensor.matmul_mx(
+                out=bank[:],
+                lhsT=q_codes[:].bitcast(FP8X4),
+                lhsT_scale=q_plane[:],
+                rhs=words[c][:, first : first + N_PASS].bitcast(FP8X4),
+                rhs_scale=key_plane[:, cols],
+                start=True,
+                stop=True,
+            )
+            if n % 2 == 0:
+                nc.scalar.copy(out=scores[:, cols], in_=bank[:])
+            else:
+                nc.vector.tensor_copy(out=scores[:, cols], in_=bank[:])
+
+        halves = [slice(h * HALF, (h + 1) * HALF) for h in range(2)]
+        entries = [slice(h * HALF // GROUP, (h + 1) * HALF // GROUP) for h in range(2)]
+        g1 = sb.tile([P, SLOTS], F32)
+        g2 = sb.tile([P, SLOTS], F32)
+        g3 = sb.tile([P, SLOTS], F32)
+        gap = sb.tile([P, SLOTS], F32)
+        capped = sb.tile([P, SLOTS], F32)
+        expo = sb.tile([P, SLOTS], F32)
+        base = sb.tile([P, SLOTS], F32)
+        part = sb.tile([P, SLOTS], F32)
+        logs = sb.tile([P, SLOTS], F32)
+        tail = sb.tile([P, SLOTS], F32)
+
+        for h in range(2):
+            nc.scalar.activation(g3[:, halves[h]], scores[:].indirect(list3[:, entries[h]]), ACT.Copy)
+            nc.vector.tensor_copy(g2[:, halves[h]], scores[:].indirect(list2[:, entries[h]]))
+        for h in range(2):
+            nc.vector.tensor_tensor(gap[:, halves[h]], g2[:, halves[h]], g3[:, halves[h]], ALU.subtract)
+            nc.vector.tensor_scalar_min(capped[:, halves[h]], gap[:, halves[h]], CLAMP)
+            nc.scalar.activation(expo[:, halves[h]], capped[:, halves[h]], ACT.Exp)
+        nc.vector.tensor_copy(g1[:], scores[:].indirect(list1[:]))
+        nc.vector.tensor_tensor(base[:], g2[:], capped[:], ALU.subtract)
+        nc.vector.scalar_tensor_tensor(part[:], base[:], neg_lam[:], g1[:], ALU.mult, ALU.add)
+        for h in range(2):
+            nc.scalar.activation(logs[:, halves[h]], expo[:, halves[h]], ACT.Ln, bias=1.0)
+            nc.scalar.activation(tail[:, halves[h]], logs[:, halves[h]], ACT.Copy, scale=neg_lam[:])
+            nc.vector.tensor_tensor(
+                window[:].indirect(list4[:, entries[h]]), part[:, halves[h]], tail[:, halves[h]], ALU.add
+            )
+
+        total = sb.tile([P, T], F32)
+        for n in range(T // STORE):
+            cols = slice(n * STORE, (n + 1) * STORE)
+            nc.vector.tensor_tensor(total[:, cols], window[:, cols], old_sb[:, cols], ALU.add)
+            queue = nc.sync if n % 2 == 0 else nc.scalar
+            queue.dma_start(out=out[:, cols], in_=total[:, cols])

@@ -18,8 +18,8 @@ D, T, SLOTS, Q = 512, 1024, 512, 128
 HALF = SLOTS // 2
 GROUP = 16
 N_PASS = 256
-CLAMP = 30.0
-STORE = 256
+PASSES = (256, 256, 256, 128, 128)
+STORES = (128, 256, 256, 256, 128)
 
 FLOPS = 2 * D * T * Q
 
@@ -32,25 +32,24 @@ def tile_attend_tworivals_lean_putold_heads_kernel(
         sb = ctx.enter_context(tc.tile_pool(name="sb", bufs=1))
         ps = ctx.enter_context(tc.psum_pool(name="ps", bufs=1))
 
-        key_plane = sb.tile([P, T], U8, align_bytes=64)
+        key_plane = sb.tile([P, N_PASS], U8, align_bytes=64)
         nc.vector.memset(key_plane[:].bitcast(I32), 0)
         window = sb.tile([P, T], F32)
         nc.vector.memset(window[:], 0.0)
 
         q_raw = sb.tile([P, PACK, Q], F32)
         nc.sync.dma_start(out=q_raw[:], in_=query.rearrange("(p j) q -> p j q", j=PACK))
+        scales_hbm = keys_scales[0].bitcast(I32).rearrange("f (n c) -> n f c", n=T // N_PASS)
+        for quad in range(4):
+            queue = nc.sync if quad < 2 else nc.scalar
+            queue.dma_start(
+                out=key_plane[32 * quad : 32 * quad + 16, :].bitcast(I32),
+                in_=scales_hbm[:, 4 * quad : 4 * quad + 4, :],
+            )
         words_hbm = keys_words[0].rearrange("p n t -> p (n t)").bitcast(I32)
         words = [sb.tile([P, T // 2], U32, align_bytes=64, name="words%d" % c) for c in range(2)]
         for c in range(2):
             nc.sync.dma_start(out=words[c][:].bitcast(I32), in_=words_hbm[:, c * (T // 2) : (c + 1) * (T // 2)])
-
-        lam_col = sb.tile([P, 1], F32)
-        nc.scalar.dma_start(out=lam_col[:], in_=lam)
-        for quad in range(4):
-            nc.scalar.dma_start(
-                out=key_plane[32 * quad : 32 * quad + 4, :].bitcast(I32),
-                in_=keys_scales[0][4 * quad : 4 * quad + 4, :].bitcast(I32),
-            )
 
         list3 = sb.tile([P, SLOTS // GROUP], U16)
         list2 = sb.tile([P, SLOTS // GROUP], U16)
@@ -61,69 +60,86 @@ def tile_attend_tworivals_lean_putold_heads_kernel(
         old_sb = sb.tile([P, T], F32)
         nc.sync.dma_start(out=old_sb[:], in_=old)
 
+        lam_col = sb.tile([P, 1], F32)
+        nc.gpsimd.dma_start(out=lam_col[:], in_=lam)
         neg_lam = sb.tile([P, 1], F32)
-        nc.scalar.activation(neg_lam[:], lam_col[:], ACT.Copy, scale=-1.0)
+        nc.gpsimd.tensor_scalar(neg_lam[:], lam_col[:], -1.0, 0.0, ALU.mult, ALU.add)
 
         q_grouped = sb.tile([P, Q, PACK], BF16, align_bytes=64)
-        nc.vector.tensor_copy(out=q_grouped[:], in_=q_raw[:].rearrange("p j q -> p q j"))
         q_codes = sb.tile([P, Q], U32, align_bytes=64)
         q_plane = sb.tile([P, Q], U8, align_bytes=64)
-        nc.vector.quantize_mx(
-            out=q_codes[:].bitcast(FP8X4), scales=q_plane[:], in_=q_grouped[:].rearrange("p q j -> p (q j)")
-        )
+        q_parts = [slice(h * Q // 2, (h + 1) * Q // 2) for h in range(2)]
+        for rows in q_parts:
+            nc.vector.tensor_copy(
+                out=q_grouped[:, rows, :].rearrange("p (c i) j -> p c j i", i=4),
+                in_=q_raw[:, :, rows].rearrange("p j (c i) -> p c j i", i=4),
+            )
+        for rows in q_parts:
+            nc.vector.quantize_mx(
+                out=q_codes[:, rows].bitcast(FP8X4),
+                scales=q_plane[:, rows],
+                in_=q_grouped[:, rows, :].rearrange("p q j -> p (q j)"),
+            )
 
         scores = sb.tile([P, T], F32)
-        for n in range(T // N_PASS):
-            bank = ps.tile([P, N_PASS], F32, name="bank%d" % n)
-            c, first = divmod(n * N_PASS, T // 2)
-            cols = slice(n * N_PASS, (n + 1) * N_PASS)
+        first = 0
+        for n, width in enumerate(PASSES):
+            bank = ps.tile([P, width], F32, name="bank%d" % n)
+            c, in_words = divmod(first, T // 2)
+            quarter, in_plane = divmod(first, N_PASS)
             nc.tensor.matmul_mx(
                 out=bank[:],
                 lhsT=q_codes[:].bitcast(FP8X4),
                 lhsT_scale=q_plane[:],
-                rhs=words[c][:, first : first + N_PASS].bitcast(FP8X4),
-                rhs_scale=key_plane[:, cols],
+                rhs=words[c][:, in_words : in_words + width].bitcast(FP8X4),
+                rhs_scale=key_plane[4 * quarter : P, in_plane : in_plane + width],
                 start=True,
                 stop=True,
             )
-            if n % 2 == 0:
-                nc.scalar.copy(out=scores[:, cols], in_=bank[:])
-            else:
-                nc.vector.tensor_copy(out=scores[:, cols], in_=bank[:])
+            copy_out = nc.scalar.copy if n % 2 == 0 else nc.vector.tensor_copy
+            copy_out(out=scores[:, first : first + width], in_=bank[:])
+            first = first + width
 
         halves = [slice(h * HALF, (h + 1) * HALF) for h in range(2)]
         entries = [slice(h * HALF // GROUP, (h + 1) * HALF // GROUP) for h in range(2)]
-        g1 = sb.tile([P, SLOTS], F32)
         g2 = sb.tile([P, SLOTS], F32)
         g3 = sb.tile([P, SLOTS], F32)
         gap = sb.tile([P, SLOTS], F32)
-        capped = sb.tile([P, SLOTS], F32)
-        expo = sb.tile([P, SLOTS], F32)
-        base = sb.tile([P, SLOTS], F32)
+        slope = sb.tile([P, SLOTS], F32)
+        top = sb.tile([P, SLOTS], F32)
+        size = sb.tile([P, HALF], F32)
         part = sb.tile([P, SLOTS], F32)
         logs = sb.tile([P, SLOTS], F32)
         tail = sb.tile([P, SLOTS], F32)
 
+        nc.scalar.activation(g3[:], scores[:].indirect(list3[:]), ACT.Copy)
         for h in range(2):
-            nc.scalar.activation(g3[:, halves[h]], scores[:].indirect(list3[:, entries[h]]), ACT.Copy)
             nc.vector.tensor_copy(g2[:, halves[h]], scores[:].indirect(list2[:, entries[h]]))
         for h in range(2):
             nc.vector.tensor_tensor(gap[:, halves[h]], g2[:, halves[h]], g3[:, halves[h]], ALU.subtract)
-            nc.vector.tensor_scalar_min(capped[:, halves[h]], gap[:, halves[h]], CLAMP)
-            nc.scalar.activation(expo[:, halves[h]], capped[:, halves[h]], ACT.Exp)
-        nc.vector.tensor_copy(g1[:], scores[:].indirect(list1[:]))
-        nc.vector.tensor_tensor(base[:], g2[:], capped[:], ALU.subtract)
-        nc.vector.scalar_tensor_tensor(part[:], base[:], neg_lam[:], g1[:], ALU.mult, ALU.add)
-        for h in range(2):
-            nc.scalar.activation(logs[:, halves[h]], expo[:, halves[h]], ACT.Ln, bias=1.0)
-            nc.scalar.activation(tail[:, halves[h]], logs[:, halves[h]], ACT.Copy, scale=neg_lam[:])
-            nc.vector.tensor_tensor(
-                window[:].indirect(list4[:, entries[h]]), part[:, halves[h]], tail[:, halves[h]], ALU.add
-            )
+            nc.scalar.activation(slope[:, halves[h]], gap[:, halves[h]], ACT.Tanh, scale=0.5)
+        nc.vector.tensor_tensor(top[:], g2[:], g3[:], ALU.max)
+        g1 = gap
+        pieces = [[slice(0, HALF)], [slice(0, HALF // 2), slice(HALF // 2, HALF)]]
+        for h in (1, 0):
+            cols = halves[h]
+            if h == 1:
+                nc.vector.scalar_tensor_tensor(size[:], slope[:, cols], -1.0, slope[:, cols], ALU.mult, ALU.max)
+            else:
+                nc.scalar.activation(size[:], slope[:, cols], ACT.Abs)
+            nc.vector.tensor_copy(g1[:, cols], scores[:].indirect(list1[:, entries[h]]))
+            nc.vector.scalar_tensor_tensor(part[:, cols], top[:, cols], neg_lam[:], g1[:, cols], ALU.mult, ALU.add)
+            for piece in pieces[h]:
+                nc.scalar.activation(logs[:, cols][:, piece], size[:, piece], ACT.Ln, bias=0.5, scale=0.5)
+            for piece in pieces[h]:
+                nc.scalar.activation(tail[:, cols][:, piece], logs[:, cols][:, piece], ACT.Copy, scale=lam_col[:])
+            nc.vector.tensor_tensor(window[:].indirect(list4[:, entries[h]]), part[:, cols], tail[:, cols], ALU.add)
 
         total = sb.tile([P, T], F32)
-        for n in range(T // STORE):
-            cols = slice(n * STORE, (n + 1) * STORE)
+        first = 0
+        for n, width in enumerate(STORES):
+            cols = slice(first, first + width)
+            first = first + width
             nc.vector.tensor_tensor(total[:, cols], window[:, cols], old_sb[:, cols], ALU.add)
             queue = nc.sync if n % 2 == 0 else nc.scalar
             queue.dma_start(out=out[:, cols], in_=total[:, cols])

@@ -18,6 +18,7 @@ D, T, SLOTS, Q = 512, 1024, 512, 128
 HALF = SLOTS // 2
 GROUP = 16
 N_PASS = 256
+LOADS = (256, 256, 512)
 PASSES = (256, 256, 256, 128, 128)
 STORES = (128, 256, 256, 256, 128)
 
@@ -47,9 +48,14 @@ def tile_attend_tworivals_lean_putold_heads_kernel(
                 in_=scales_hbm[:, 4 * quad : 4 * quad + 4, :],
             )
         words_hbm = keys_words[0].rearrange("p n t -> p (n t)").bitcast(I32)
-        words = [sb.tile([P, T // 2], U32, align_bytes=64, name="words%d" % c) for c in range(2)]
-        for c in range(2):
-            nc.sync.dma_start(out=words[c][:].bitcast(I32), in_=words_hbm[:, c * (T // 2) : (c + 1) * (T // 2)])
+        word_of = {}
+        first = 0
+        for c, width in enumerate(LOADS):
+            chunk = sb.tile([P, width], U32, align_bytes=64, name="words%d" % c)
+            nc.sync.dma_start(out=chunk[:].bitcast(I32), in_=words_hbm[:, first : first + width])
+            for col in range(0, width, 128):
+                word_of[first + col] = (chunk, col)
+            first = first + width
 
         list3 = sb.tile([P, SLOTS // GROUP], U16)
         list2 = sb.tile([P, SLOTS // GROUP], U16)
@@ -85,13 +91,13 @@ def tile_attend_tworivals_lean_putold_heads_kernel(
         first = 0
         for n, width in enumerate(PASSES):
             bank = ps.tile([P, width], F32, name="bank%d" % n)
-            c, in_words = divmod(first, T // 2)
+            chunk, in_words = word_of[first]
             quarter, in_plane = divmod(first, N_PASS)
             nc.tensor.matmul_mx(
                 out=bank[:],
                 lhsT=q_codes[:].bitcast(FP8X4),
                 lhsT_scale=q_plane[:],
-                rhs=words[c][:, in_words : in_words + width].bitcast(FP8X4),
+                rhs=chunk[:, in_words : in_words + width].bitcast(FP8X4),
                 rhs_scale=key_plane[4 * quarter : P, in_plane : in_plane + width],
                 start=True,
                 stop=True,
@@ -102,7 +108,7 @@ def tile_attend_tworivals_lean_putold_heads_kernel(
 
         halves = [slice(h * HALF, (h + 1) * HALF) for h in range(2)]
         entries = [slice(h * HALF // GROUP, (h + 1) * HALF // GROUP) for h in range(2)]
-        g2 = sb.tile([P, SLOTS], F32)
+        g2 = sb.tile([P, HALF], F32)
         g3 = sb.tile([P, SLOTS], F32)
         gap = sb.tile([P, SLOTS], F32)
         slope = sb.tile([P, SLOTS], F32)
@@ -112,18 +118,19 @@ def tile_attend_tworivals_lean_putold_heads_kernel(
         logs = sb.tile([P, SLOTS], F32)
         tail = sb.tile([P, SLOTS], F32)
 
-        nc.scalar.activation(g3[:], scores[:].indirect(list3[:]), ACT.Copy)
-        for h in range(2):
-            nc.vector.tensor_copy(g2[:, halves[h]], scores[:].indirect(list2[:, entries[h]]))
-        for h in range(2):
-            nc.vector.tensor_tensor(gap[:, halves[h]], g2[:, halves[h]], g3[:, halves[h]], ALU.subtract)
-            nc.scalar.activation(slope[:, halves[h]], gap[:, halves[h]], ACT.Tanh, scale=0.5)
-        nc.vector.tensor_tensor(top[:], g2[:], g3[:], ALU.max)
-        g1 = gap
-        pieces = [[slice(0, HALF)], [slice(0, HALF // 2), slice(HALF // 2, HALF)]]
         for h in (1, 0):
+            nc.scalar.activation(g3[:, halves[h]], scores[:].indirect(list3[:, entries[h]]), ACT.Copy)
+        nc.vector.tensor_copy(g2[:], scores[:].indirect(list2[:, entries[0]]))
+        minuends = [g2[:], scores[:].indirect(list2[:, entries[1]])]
+        for h in (1, 0):
+            nc.vector.tensor_tensor(gap[:, halves[h]], minuends[h], g3[:, halves[h]], ALU.subtract)
+            nc.scalar.activation(slope[:, halves[h]], gap[:, halves[h]], ACT.Tanh, scale=0.5)
+        nc.vector.scalar_tensor_tensor(top[:], gap[:], 0.0, g3[:], ALU.max, ALU.add)
+        g1 = gap
+        pieces = [[slice(0, HALF // 2), slice(HALF // 2, HALF)], [slice(0, HALF)]]
+        for h in range(2):
             cols = halves[h]
-            if h == 1:
+            if h == 0:
                 nc.vector.scalar_tensor_tensor(size[:], slope[:, cols], -1.0, slope[:, cols], ALU.mult, ALU.max)
             else:
                 nc.scalar.activation(size[:], slope[:, cols], ACT.Abs)

from contextlib import ExitStack

import concourse.mybir as mybir

F32 = mybir.dt.float32
BF16 = mybir.dt.bfloat16
I32 = mybir.dt.int32
U32 = mybir.dt.uint32
U16 = mybir.dt.uint16
U8 = mybir.dt.uint8
FP8X4 = mybir.dt.float8_e4m3fn_x4
ALU = mybir.AluOpType
ACT = mybir.ActivationFunctionType

P = 128
PACK = 4
D, T, SLOTS, Q = 512, 1024, 512, 128
HALF = SLOTS // 2
GROUP = 16
N_PASS = 256
LOADS = (256, 256, 512)
PASSES = (256, 256, 256, 128, 128)
STORES = (128, 256, 256, 256, 128)

FLOPS = 2 * D * T * Q


def tile_attend_tworivals_lean_putold_heads_kernel(
    tc, query, keys_words, keys_scales, lam, old, offs, offs2, offs3, offs4, out
):
    nc = tc.nc
    with ExitStack() as ctx:
        sb = ctx.enter_context(tc.tile_pool(name="sb", bufs=1))
        ps = ctx.enter_context(tc.psum_pool(name="ps", bufs=1))

        key_plane = sb.tile([P, N_PASS], U8, align_bytes=64)
        nc.vector.memset(key_plane[:].bitcast(I32), 0)
        window = sb.tile([P, T], F32)
        nc.vector.memset(window[:], 0.0)

        q_raw = sb.tile([P, PACK, Q], F32)
        nc.sync.dma_start(out=q_raw[:], in_=query.rearrange("(p j) q -> p j q", j=PACK))
        scales_hbm = keys_scales[0].bitcast(I32).rearrange("f (n c) -> n f c", n=T // N_PASS)
        for quad in range(4):
            queue = nc.sync if quad < 2 else nc.scalar
            queue.dma_start(
                out=key_plane[32 * quad : 32 * quad + 16, :].bitcast(I32),
                in_=scales_hbm[:, 4 * quad : 4 * quad + 4, :],
            )
        words_hbm = keys_words[0].rearrange("p n t -> p (n t)").bitcast(I32)
        word_of = {}
        first = 0
        for c, width in enumerate(LOADS):
            chunk = sb.tile([P, width], U32, align_bytes=64, name="words%d" % c)
            nc.sync.dma_start(out=chunk[:].bitcast(I32), in_=words_hbm[:, first : first + width])
            for col in range(0, width, 128):
                word_of[first + col] = (chunk, col)
            first = first + width

        list3 = sb.tile([P, SLOTS // GROUP], U16)
        list2 = sb.tile([P, SLOTS // GROUP], U16)
        list1 = sb.tile([P, SLOTS // GROUP], U16)
        list4 = sb.tile([P, SLOTS // GROUP], U16)
        for lst, src in ((list3, offs3), (list2, offs2), (list1, offs), (list4, offs4)):
            nc.sync.dma_start(lst[:], src)
        old_sb = sb.tile([P, T], F32)
        nc.sync.dma_start(out=old_sb[:], in_=old)

        lam_col = sb.tile([P, 1], F32)
        nc.gpsimd.dma_start(out=lam_col[:], in_=lam)
        neg_lam = sb.tile([P, 1], F32)
        nc.gpsimd.tensor_scalar(neg_lam[:], lam_col[:], -1.0, 0.0, ALU.mult, ALU.add)

        q_grouped = sb.tile([P, Q, PACK], BF16, align_bytes=64)
        q_codes = sb.tile([P, Q], U32, align_bytes=64)
        q_plane = sb.tile([P, Q], U8, align_bytes=64)
        q_parts = [slice(h * Q // 2, (h + 1) * Q // 2) for h in range(2)]
        for rows in q_parts:
            nc.vector.tensor_copy(
                out=q_grouped[:, rows, :].rearrange("p (c i) j -> p c j i", i=4),
                in_=q_raw[:, :, rows].rearrange("p j (c i) -> p c j i", i=4),
            )
        for rows in q_parts:
            nc.vector.quantize_mx(
                out=q_codes[:, rows].bitcast(FP8X4),
                scales=q_plane[:, rows],
                in_=q_grouped[:, rows, :].rearrange("p q j -> p (q j)"),
            )

        scores = sb.tile([P, T], F32)
        first = 0
        for n, width in enumerate(PASSES):
            bank = ps.tile([P, width], F32, name="bank%d" % n)
            chunk, in_words = word_of[first]
            quarter, in_plane = divmod(first, N_PASS)
            nc.tensor.matmul_mx(
                out=bank[:],
                lhsT=q_codes[:].bitcast(FP8X4),
                lhsT_scale=q_plane[:],
                rhs=chunk[:, in_words : in_words + width].bitcast(FP8X4),
                rhs_scale=key_plane[4 * quarter : P, in_plane : in_plane + width],
                start=True,
                stop=True,
            )
            copy_out = nc.scalar.copy if n % 2 == 0 else nc.vector.tensor_copy
            copy_out(out=scores[:, first : first + width], in_=bank[:])
            first = first + width

        halves = [slice(h * HALF, (h + 1) * HALF) for h in range(2)]
        entries = [slice(h * HALF // GROUP, (h + 1) * HALF // GROUP) for h in range(2)]
        g2 = sb.tile([P, HALF], F32)
        g3 = sb.tile([P, SLOTS], F32)
        gap = sb.tile([P, SLOTS], F32)
        slope = sb.tile([P, SLOTS], F32)
        top = sb.tile([P, SLOTS], F32)
        size = sb.tile([P, HALF], F32)
        part = sb.tile([P, SLOTS], F32)
        logs = sb.tile([P, SLOTS], F32)
        tail = sb.tile([P, SLOTS], F32)

        for h in (1, 0):
            nc.scalar.activation(g3[:, halves[h]], scores[:].indirect(list3[:, entries[h]]), ACT.Copy)
        nc.vector.tensor_copy(g2[:], scores[:].indirect(list2[:, entries[0]]))
        minuends = [g2[:], scores[:].indirect(list2[:, entries[1]])]
        for h in (1, 0):
            nc.vector.tensor_tensor(gap[:, halves[h]], minuends[h], g3[:, halves[h]], ALU.subtract)
            nc.scalar.activation(slope[:, halves[h]], gap[:, halves[h]], ACT.Tanh, scale=0.5)
        nc.vector.scalar_tensor_tensor(top[:], gap[:], 0.0, g3[:], ALU.max, ALU.add)
        g1 = gap
        pieces = [[slice(0, HALF // 2), slice(HALF // 2, HALF)], [slice(0, HALF)]]
        for h in range(2):
            cols = halves[h]
            if h == 0:
                nc.vector.scalar_tensor_tensor(size[:], slope[:, cols], -1.0, slope[:, cols], ALU.mult, ALU.max)
            else:
                nc.scalar.activation(size[:], slope[:, cols], ACT.Abs)
            nc.vector.tensor_copy(g1[:, cols], scores[:].indirect(list1[:, entries[h]]))
            nc.vector.scalar_tensor_tensor(part[:, cols], top[:, cols], neg_lam[:], g1[:, cols], ALU.mult, ALU.add)
            for piece in pieces[h]:
                nc.scalar.activation(logs[:, cols][:, piece], size[:, piece], ACT.Ln, bias=0.5, scale=0.5)
            for piece in pieces[h]:
                nc.scalar.activation(tail[:, cols][:, piece], logs[:, cols][:, piece], ACT.Copy, scale=lam_col[:])
            nc.vector.tensor_tensor(window[:].indirect(list4[:, entries[h]]), part[:, cols], tail[:, cols], ALU.add)

        total = sb.tile([P, T], F32)
        first = 0
        for n, width in enumerate(STORES):
            cols = slice(first, first + width)
            first = first + width
            nc.vector.tensor_tensor(total[:, cols], window[:, cols], old_sb[:, cols], ALU.add)
            queue = nc.sync if n % 2 == 0 else nc.scalar
            queue.dma_start(out=out[:, cols], in_=total[:, cols])
